import numpy as np
import ml_dtypes


def mxq(x, axis, fmt="e4m3"):
    dtype, down = {"e4m3": (ml_dtypes.float8_e4m3fn, 7), "e5m2": (ml_dtypes.float8_e5m2, 14)}[fmt]
    v = np.moveaxis(np.asarray(x, np.float32).astype(ml_dtypes.bfloat16).astype(np.float64), axis, -1)
    blocks = v.reshape(v.shape[:-1] + (-1, 32))
    amax = np.abs(blocks).max(-1, keepdims=True)
    byte = np.maximum(np.where(amax > 0, np.frexp(amax)[1] - 1 + 127, 0) - down, 1)
    scale = np.exp2(byte - 127.0)
    codes = (blocks / scale).astype(np.float32).astype(dtype).astype(np.float64)
    return np.moveaxis((codes * scale).reshape(v.shape), -1, axis)


WIDE = False


def mx_kscale(k):
    if not WIDE:
        return np.ones(k)
    levels = np.array([10, -10, 5, -5, 0])
    if k % 512:
        return np.exp2(np.random.permutation(np.resize(levels, k // 32))).repeat(32)
    a = np.empty((k // 512, 16))
    for p in range(k // 512):
        a[p, :8] = np.random.permutation(np.resize(levels, 8))
        for g in range(8):
            far = levels[np.abs(levels - a[p, g]) >= 10]
            a[p, g + 8] = far[np.random.randint(len(far))]
    return np.exp2(a.ravel()).repeat(32)


def f64(x):
    return np.asarray(x).astype(np.float64)


def striped(idx):
    return np.tile(idx.reshape(-1, 16).T, (8, 1)).astype(np.uint16)


def unstriped(offs):
    return offs[:16].T.reshape(-1).astype(np.int64)


def pack_weight(w):
    k, n = w.shape
    w = f64(np.asarray(w, np.float32).astype(ml_dtypes.bfloat16)).reshape(k // 32, 32, n)
    amax = np.abs(w).max(1)
    byte = np.clip(np.where(amax > 0, np.frexp(amax)[1] - 1 + 127 - 7, 1), 1, 254)
    scaled = (w * np.exp2(127.0 - byte)[:, None, :]).reshape(k, n).astype(np.float32)
    words = np.ascontiguousarray(scaled.reshape(k // 512, 128, 4, n).transpose(0, 1, 3, 2)).astype(ml_dtypes.float8_e4m3fn).view(np.uint8)
    return words, np.ascontiguousarray(byte.astype(np.uint8).reshape(k // 512, 16, n))


def unpack_weight(words, scales):
    g, p, n, _ = words.shape
    vals = np.ascontiguousarray(words).view(ml_dtypes.float8_e4m3fn).astype(np.float64) * np.repeat(np.exp2(scales.astype(np.float64) - 127.0), 8, axis=1)[..., None]
    return vals.transpose(0, 1, 3, 2).reshape(g * 512, n)


E2M1 = np.array([0.0, 0.5, 1.0, 1.5, 2.0, 3.0, 4.0, 6.0, -0.0, -0.5, -1.0, -1.5, -2.0, -3.0, -4.0, -6.0])


def pack_fp4(w):
    k, n = w.shape
    w = f64(np.asarray(w, np.float32).astype(ml_dtypes.bfloat16)).reshape(k // 32, 32, n)
    amax = np.abs(w).max(1)
    mant, ex = np.frexp(amax / 6.0)
    byte = np.clip(np.where(amax > 0, np.where(mant > 0.5, ex, ex - 1) + 127, 1), 1, 254)
    scaled = (w * np.exp2(127.0 - byte)[:, None, :]).reshape(k, n).astype(np.float32)
    c = np.ascontiguousarray(scaled.reshape(k // 512, 128, 4, n).transpose(0, 1, 3, 2)).astype(ml_dtypes.float4_e2m1fn).view(np.uint8) & 0xF
    words = (c[..., 0::2] | (c[..., 1::2] << 4)).reshape(k // 512, 128, 2 * n)
    return np.ascontiguousarray(words), np.ascontiguousarray(byte.astype(np.uint8).reshape(k // 512, 16, n))


def unpack_fp4(words, scales):
    g, _, n = scales.shape
    words = np.ascontiguousarray(words).reshape(g, 128, n, 2)
    nib = np.empty((g, 128, n, 4), np.uint8)
    nib[..., 0::2] = words & 0xF
    nib[..., 1::2] = words >> 4
    vals = E2M1[nib] * np.repeat(np.exp2(scales.astype(np.float64) - 127.0), 8, axis=1)[..., None]
    return vals.transpose(0, 1, 3, 2).reshape(g * 512, n)


K, T, S, D, N, H = 1024, 4096, 1024, 4, 128, 512


def setup_inputs():
    n = np.random.standard_normal
    s = mx_kscale(K)[:, None]
    u = mx_kscale(H)
    packed_xT = pack_weight(n((K, T)) * s)
    packed_w1 = pack_fp4(n((K, H)) / np.sqrt(K) / s)
    packed_w2 = pack_fp4(n((H, N)) / np.sqrt(H) / u[:, None])
    return {
        "x_words": packed_xT[0],
        "x_scales": packed_xT[1],
        "w1_words": packed_w1[0],
        "w1_scales": packed_w1[1],
        "bid": (np.random.uniform(0.2, 1.0, (H, S))).astype(np.float32),
        "unit": (np.random.uniform(0.6, 1.4, (H, 1)) * u[:, None]).astype(np.float32),
        "w2_words": packed_w2[0],
        "w2_scales": packed_w2[1],
        "offs": striped(np.random.permutation(T)[:S]),
        "good": striped(np.random.permutation(S)),
    }


def reference(x_words, x_scales, w1_words, w1_scales, bid, unit, w2_words, w2_scales, offs, good):
    bgd = f64(bid)[:, unstriped(good)]
    price = bgd.reshape(len(bgd), -1, D).sum(axis=2) + 0.2
    alloc = bgd / np.repeat(price, D, axis=1)
    xq = unpack_weight(x_words, x_scales)[:, unstriped(offs)]
    y = unpack_fp4(w1_words, w1_scales).T @ xq
    val = np.exp(0.9 * np.tanh(y))
    vg = val[:, unstriped(good)]
    util = alloc * vg
    hid = f64(unit) * (util * (np.log(np.repeat(price, D, axis=1))))
    return unpack_fp4(w2_words, w2_scales).T @ mxq(hid, 0, "e4m3")

@@ -1,0 +1,255 @@
+from contextlib import ExitStack
+
+import concourse.mybir as mybir
+
+K, T, S, D, N, H = 1024, 4096, 1024, 4, 128, 512
+FLOPS = 2 * K * H * S + 2 * H * N * S
+
+F32 = mybir.dt.float32
+BF16 = mybir.dt.bfloat16
+I32 = mybir.dt.int32
+U32 = mybir.dt.uint32
+U16 = mybir.dt.uint16
+U8 = mybir.dt.uint8
+FP8X4 = mybir.dt.float8_e4m3fn_x4
+FP4X4 = mybir.dt.float4_e2m1fn_x4
+ACT = mybir.ActivationFunctionType
+ALU = mybir.AluOpType
+
+P = 128
+PACK = 4
+PASSES = K // (P * PACK)
+HALF = S // 2
+GROUPS = S // D
+QUADS = 4
+LIST_COLS = S // 16
+TOP = 96
+
+
+def tile_picked_yfishm_log_p_kernel(
+    tc, x_words, x_scales, w1_words, w1_scales, bid, unit, w2_words, w2_scales, offs, good, out
+):
+    nc = tc.nc
+    with ExitStack() as ctx:
+        lists = ctx.enter_context(tc.tile_pool(name="lists", bufs=1))
+        keep = ctx.enter_context(tc.tile_pool(name="keep", bufs=1))
+        psum = ctx.enter_context(tc.psum_pool(name="psum", bufs=1))
+
+        def sb(name, shape, dtype):
+            return keep.tile(shape, dtype, name=name, align_bytes=64)
+
+        good_sb = lists.tile([P, LIST_COLS], U16, name="good_sb")
+        offs_sb = lists.tile([P, LIST_COLS], U16, name="offs_sb")
+
+        def entries(list_sb, lo, hi):
+            return list_sb[:, lo // 16 : hi // 16]
+
+        xs_table = sb("xs_table", [P, T], U8)
+        w1s_raw = sb("w1s_raw", [P, H], U8)
+        w2s = sb("w2s", [P, N], U8)
+        xs_planes = sb("xs_planes", [P, PASSES * S], U8)
+        w1s_planes = sb("w1s_planes", [P, PASSES * H], U8)
+        for table in (xs_table, w1s_raw):
+            nc.vector.memset(table[0:TOP, :].bitcast(I32), 0)
+        for plane in (xs_planes, w1s_planes, w2s):
+            nc.vector.memset(plane[:].bitcast(I32), 0)
+
+        nc.sync.dma_start(offs_sb[:], offs)
+        nc.sync.dma_start(xs_table[TOP:P, :].bitcast(I32), x_scales.bitcast(I32).rearrange("o s c -> s o c"))
+        nc.sync.dma_start(good_sb[:], good)
+        bid_rows = bid.rearrange("(p t) j -> p t j", t=PACK)
+        bid_sb = [sb(f"bid{t}", [P, S], F32) for t in range(PACK)]
+        nc.sync.dma_start(bid_sb[0][:], bid_rows[:, 0, :])
+        nc.sync.dma_start(w1s_raw[TOP:P, :].bitcast(I32), w1_scales.bitcast(I32).rearrange("o s c -> s o c"))
+        for t in range(1, PACK):
+            nc.sync.dma_start(bid_sb[t][:], bid_rows[:, t, :])
+        w1_raw = sb("w1_raw", [P, PASSES * 2 * H], U8)
+        nc.sync.dma_start(
+            w1_raw[:].bitcast(I32).rearrange("p (o c) -> p o c", o=PASSES),
+            w1_words.bitcast(I32).rearrange("o p c -> p o c"),
+        )
+        unit_sb = sb("unit_sb", [P, PACK], F32)
+        nc.sync.dma_start(unit_sb[:], unit.rearrange("(p t) o -> p (t o)", t=PACK))
+        x_table = [sb(f"x_table{o}", [P, T], I32) for o in range(PASSES)]
+        for o in range(PASSES):
+            nc.sync.dma_start(x_table[o][:], x_words[o].rearrange("p c r -> p (c r)").bitcast(I32))
+        w2_sb = sb("w2_sb", [P, 2 * N], U8)
+        nc.sync.dma_start(w2_sb[:].bitcast(I32), w2_words[0].bitcast(I32))
+        for q in range(QUADS):
+            nc.sync.dma_start(w2s[32 * q : 32 * q + 4, :].bitcast(I32), w2_scales[0, 4 * q : 4 * q + 4, :].bitcast(I32))
+
+        def place_scale_rows(planes, rows):
+            for q in range(QUADS):
+                nc.gpsimd.dma_start(
+                    planes[32 * q : 32 * q + 4, :].bitcast(I32).rearrange("r (o c) -> r o c", o=PASSES),
+                    rows[TOP + 8 * q : TOP + 8 * q + 8, :].bitcast(I32),
+                )
+
+        xs_picked = sb("xs_picked", [P, S], U8)
+        nc.vector.tensor_copy(xs_picked[:], xs_table[:].indirect(offs_sb[:]))
+        place_scale_rows(xs_planes, xs_picked)
+        w1s_dealt = sb("w1s_dealt", [P, H], U8)
+        nc.vector.tensor_copy(
+            w1s_dealt[:].rearrange("p (t m) -> p t m", t=PACK),
+            w1s_raw[:].rearrange("p (m t) -> p t m", t=PACK),
+        )
+        place_scale_rows(w1s_planes, w1s_dealt)
+
+        bgd = [sb(f"bgd{t}", [P, S], F32) for t in range(PACK)]
+        total = sb("total", [P, PACK * GROUPS], F32)
+        pairs = [sb(f"pairs{t}", [P, 2 * GROUPS], F32) for t in range(PACK)]
+
+        def gather_bids(t, h, on_vector):
+            window = bid_sb[t][:].indirect(entries(good_sb, h * HALF, (h + 1) * HALF))
+            dst = bgd[t][:, h * HALF : (h + 1) * HALF]
+            if on_vector:
+                nc.vector.tensor_copy(dst, window)
+            else:
+                nc.scalar.activation(dst, window, ACT.Copy)
+
+        def add_pairs(t):
+            four = bgd[t][:].rearrange("p (v d) -> p v d", d=D)
+            nc.vector.tensor_tensor(
+                pairs[t][:].rearrange("p (v e) -> p v e", e=2), four[:, :, 0:2], four[:, :, 2:4], ALU.add
+            )
+
+        def add_totals(t):
+            two = pairs[t][:].rearrange("p (v e) -> p v e", e=2)
+            nc.vector.tensor_tensor(total[:, t * GROUPS : (t + 1) * GROUPS], two[:, :, 0], two[:, :, 1], ALU.add)
+
+        for t in range(PACK):
+            gather_bids(t, 0, False)
+            gather_bids(t, 1, t > 0)
+            add_pairs(t)
+            if t > 0:
+                add_totals(t - 1)
+        add_totals(PACK - 1)
+
+        log_price = sb("log_price", [P, PACK * GROUPS], F32)
+        last = (PACK - 1) * GROUPS
+        nc.scalar.activation(log_price[:, :last], total[:, :last], ACT.Ln, bias=0.2)
+        nc.scalar.activation(log_price[:, last:], total[:, last:], ACT.Ln, bias=0.2)
+        inv_price = sb("inv_price", [P, PACK * GROUPS], F32)
+        weight = sb("weight", [P, PACK * GROUPS], F32)
+
+        def half_groups(tile, h):
+            return tile[:].rearrange("p (t h v) -> p t h v", t=PACK, h=2)[:, :, h, :]
+
+        for h in range(2):
+            nc.scalar.activation(half_groups(inv_price, h), half_groups(log_price, h), ACT.Exp, scale=-1.0)
+
+        w1_dealt = sb("w1_dealt", [P, PASSES * 2 * H], U8)
+        nc.vector.tensor_copy(
+            w1_dealt[:].bitcast(U16).rearrange("p (t g) -> p t g", t=PACK),
+            w1_raw[:].bitcast(U16).rearrange("p (g t) -> p t g", t=PACK),
+        )
+
+        x_picked = [[sb(f"x_picked{o}_{h}", [P, HALF], U32) for h in range(2)] for o in range(PASSES)]
+        y = [[psum.tile([P, HALF], F32, name=f"y{t}_{h}", tag=f"bank{t}_{h}") for h in range(2)] for t in range(PACK)]
+
+        def gather_words(o, h):
+            nc.vector.tensor_copy(
+                x_picked[o][h][:], x_table[o][:].bitcast(U32).indirect(entries(offs_sb, h * HALF, (h + 1) * HALF))
+            )
+
+        def first_product(o, t, h):
+            blk = t * PASSES + o
+            nc.tensor.matmul_mx(
+                y[t][h][:],
+                lhsT=w1_dealt[:, blk * 2 * P : (blk + 1) * 2 * P].bitcast(FP4X4),
+                lhsT_scale=w1s_planes[:, o * H + t * P : o * H + (t + 1) * P],
+                rhs=x_picked[o][h][:].bitcast(FP8X4),
+                rhs_scale=xs_planes[:, o * S + h * HALF : o * S + (h + 1) * HALF],
+                start=(o == 0),
+                stop=(o == PASSES - 1),
+            )
+
+        for h in range(2):
+            gather_words(0, h)
+            for t in range(PACK):
+                first_product(0, t, h)
+
+        for h in range(2):
+            nc.vector.tensor_tensor(half_groups(weight, h), half_groups(log_price, h), half_groups(inv_price, h), ALU.mult)
+
+        for h in range(2):
+            gather_words(1, h)
+        for tp in range(2):
+            for h in range(2):
+                for t in (2 * tp, 2 * tp + 1):
+                    first_product(1, t, h)
+
+        factor = [sb(f"factor{h}", [P, PACK, HALF], F32) for h in range(2)]
+        for h in range(2):
+            for t in range(PACK):
+                lo = t * GROUPS + h * (GROUPS // 2)
+                nc.vector.scalar_tensor_tensor(
+                    factor[h][:, t, :].rearrange("p (v d) -> p v d", d=D),
+                    bgd[t][:, h * HALF : (h + 1) * HALF].rearrange("p (v d) -> p v d", d=D),
+                    unit_sb[:, t : t + 1],
+                    weight[:, lo : lo + GROUPS // 2].unsqueeze(2).to_broadcast([P, GROUPS // 2, D]),
+                    ALU.mult,
+                    ALU.mult,
+                )
+
+        wide = [sb(f"wide{u}", [P, 2 * S], F32) for u in range(2)]
+        val = [sb(f"val{u}", [P, S], F32) for u in range(2)]
+        vg = [sb(f"vg{h}", [P, PACK, HALF], F32) for h in range(2)]
+
+        def squash(t, h):
+            lo = (S if t < 2 else 0) + h * HALF
+            nc.scalar.activation(wide[t % 2][:, lo : lo + HALF], y[t][h][:], ACT.Tanh)
+
+        def plain_exp(t):
+            nc.scalar.activation(val[t][:], wide[t][:, S:], ACT.Exp, scale=0.9)
+
+        def gather_val(t, h):
+            nc.vector.tensor_copy(vg[h][:, t, :], val[t][:].indirect(entries(good_sb, h * HALF, (h + 1) * HALF)))
+
+        def gather_exp(t, h):
+            nc.scalar.activation(
+                vg[h][:, t, :], wide[t % 2][:].indirect(entries(good_sb, h * HALF, (h + 1) * HALF)), ACT.Exp, scale=0.9
+            )
+
+        squash(0, 0)
+        squash(1, 0)
+        squash(0, 1)
+        plain_exp(0)
+        squash(1, 1)
+        plain_exp(1)
+        for t in (2, 3):
+            squash(t, 0)
+            squash(t, 1)
+            gather_exp(t, 0)
+        for t in (2, 3):
+            gather_exp(t, 1)
+        for t in (0, 1):
+            for h in range(2):
+                gather_val(t, h)
+
+        pieces = [(0, 256), (256, 256), (512, 256), (768, 128), (896, 128)]
+        for n, (lo, width) in enumerate(pieces):
+            h, c0 = divmod(lo, HALF)
+            hid = sb(f"hid{n}", [P, PACK * width], BF16)
+            nc.vector.tensor_tensor(
+                hid[:].rearrange("p (c i t) -> p c t i", i=2, t=PACK),
+                vg[h][:, :, c0 : c0 + width].rearrange("p t (c i) -> p c t i", i=2),
+                factor[h][:, :, c0 : c0 + width].rearrange("p t (c i) -> p c t i", i=2),
+                ALU.mult,
+            )
+            codes = sb(f"codes{n}", [P, width], U32)
+            scales = sb(f"scales{n}", [P, width], U8)
+            nc.vector.quantize_mx(codes[:].bitcast(FP8X4), scales[:], hid[:])
+            acc = psum.tile([P, width], F32, name=f"acc{n}", tag=f"bank{n % PACK}_{n // PACK}")
+            nc.tensor.matmul_mx(
+                acc[:],
+                lhsT=w2_sb[:].bitcast(FP4X4),
+                lhsT_scale=w2s[:],
+                rhs=codes[:].bitcast(FP8X4),
+                rhs_scale=scales[:],
+                start=True,
+                stop=True,
+            )
+            res = sb(f"res{n}", [P, width], F32)
+            nc.scalar.copy(res[:], acc[:])
+            nc.sync.dma_start(out[:, lo : lo + width], res[:])

@@ -35,8 +35,8 @@ def tile_picked_yfishm_log_p_kernel(
         keep = ctx.enter_context(tc.tile_pool(name="keep", bufs=1))
         psum = ctx.enter_context(tc.psum_pool(name="psum", bufs=1))
 
-        def sb(name, shape, dtype):
-            return keep.tile(shape, dtype, name=name, align_bytes=64)
+        def sb(name, shape, dtype, tag=None):
+            return keep.tile(shape, dtype, name=name, tag=tag or name, align_bytes=64)
 
         good_sb = lists.tile([P, LIST_COLS], U16, name="good_sb")
         offs_sb = lists.tile([P, LIST_COLS], U16, name="offs_sb")
@@ -45,55 +45,58 @@ def tile_picked_yfishm_log_p_kernel(
             return list_sb[:, lo // 16 : hi // 16]
 
         xs_table = sb("xs_table", [P, T], U8)
-        w1s_raw = sb("w1s_raw", [P, H], U8)
-        w2s = sb("w2s", [P, N], U8)
+        w1s_raw = sb("w1s_raw", [P, PASSES * H], U8)
         xs_planes = sb("xs_planes", [P, PASSES * S], U8)
-        w1s_planes = sb("w1s_planes", [P, PASSES * H], U8)
-        for table in (xs_table, w1s_raw):
-            nc.vector.memset(table[0:TOP, :].bitcast(I32), 0)
-        for plane in (xs_planes, w1s_planes, w2s):
-            nc.vector.memset(plane[:].bitcast(I32), 0)
+        nc.gpsimd.memset(w1s_raw[:].bitcast(I32), 0)
+        nc.vector.memset(xs_table[0:TOP, :].bitcast(I32), 0)
+        nc.vector.memset(xs_planes[:].bitcast(I32), 0)
 
         nc.sync.dma_start(offs_sb[:], offs)
         nc.sync.dma_start(xs_table[TOP:P, :].bitcast(I32), x_scales.bitcast(I32).rearrange("o s c -> s o c"))
         nc.sync.dma_start(good_sb[:], good)
         bid_rows = bid.rearrange("(p t) j -> p t j", t=PACK)
         bid_sb = [sb(f"bid{t}", [P, S], F32) for t in range(PACK)]
-        nc.sync.dma_start(bid_sb[0][:], bid_rows[:, 0, :])
-        nc.sync.dma_start(w1s_raw[TOP:P, :].bitcast(I32), w1_scales.bitcast(I32).rearrange("o s c -> s o c"))
-        for t in range(1, PACK):
+        for t in range(2):
+            nc.sync.dma_start(bid_sb[t][:], bid_rows[:, t, :])
+        for q in range(QUADS):
+            nc.sync.dma_start(
+                w1s_raw[32 * q : 32 * q + 4, :].bitcast(I32).rearrange("r (o c) -> r o c", o=PASSES),
+                w1_scales[:, 4 * q : 4 * q + 4, :].bitcast(I32).rearrange("o r c -> r o c"),
+            )
+        for t in range(2, PACK):
             nc.sync.dma_start(bid_sb[t][:], bid_rows[:, t, :])
         w1_raw = sb("w1_raw", [P, PASSES * 2 * H], U8)
         nc.sync.dma_start(
             w1_raw[:].bitcast(I32).rearrange("p (o c) -> p o c", o=PASSES),
             w1_words.bitcast(I32).rearrange("o p c -> p o c"),
         )
-        unit_sb = sb("unit_sb", [P, PACK], F32)
-        nc.sync.dma_start(unit_sb[:], unit.rearrange("(p t) o -> p (t o)", t=PACK))
-        x_table = [sb(f"x_table{o}", [P, T], I32) for o in range(PASSES)]
-        for o in range(PASSES):
-            nc.sync.dma_start(x_table[o][:], x_words[o].rearrange("p c r -> p (c r)").bitcast(I32))
-        w2_sb = sb("w2_sb", [P, 2 * N], U8)
-        nc.sync.dma_start(w2_sb[:].bitcast(I32), w2_words[0].bitcast(I32))
-        for q in range(QUADS):
-            nc.sync.dma_start(w2s[32 * q : 32 * q + 4, :].bitcast(I32), w2_scales[0, 4 * q : 4 * q + 4, :].bitcast(I32))
+        x_table = [None] * PASSES
 
-        def place_scale_rows(planes, rows):
-            for q in range(QUADS):
-                nc.gpsimd.dma_start(
-                    planes[32 * q : 32 * q + 4, :].bitcast(I32).rearrange("r (o c) -> r o c", o=PASSES),
-                    rows[TOP + 8 * q : TOP + 8 * q + 8, :].bitcast(I32),
-                )
+        def load_words(o, tag):
+            x_table[o] = sb(f"x_table{o}", [P, T], I32, tag=tag)
+            nc.sync.dma_start(x_table[o][:], x_words[o].rearrange("p c r -> p (c r)").bitcast(I32))
+
+        load_words(0, "x_table0")
 
         xs_picked = sb("xs_picked", [P, S], U8)
         nc.vector.tensor_copy(xs_picked[:], xs_table[:].indirect(offs_sb[:]))
-        place_scale_rows(xs_planes, xs_picked)
-        w1s_dealt = sb("w1s_dealt", [P, H], U8)
+        for q in range(QUADS):
+            nc.sync.dma_start(
+                xs_planes[32 * q : 32 * q + 4, :].bitcast(I32).rearrange("r (o c) -> r o c", o=PASSES),
+                xs_picked[TOP + 8 * q : TOP + 8 * q + 8, :].bitcast(I32),
+            )
+        load_words(1, "xs_table")
+
+        w1s_dealt = sb("w1s_dealt", [P, PASSES * H], U8)
         nc.vector.tensor_copy(
-            w1s_dealt[:].rearrange("p (t m) -> p t m", t=PACK),
-            w1s_raw[:].rearrange("p (m t) -> p t m", t=PACK),
+            w1s_dealt[:].rearrange("p (t g) -> p t g", t=PACK),
+            w1s_raw[:].rearrange("p (g t) -> p t g", t=PACK),
         )
-        place_scale_rows(w1s_planes, w1s_dealt)
+        w1_dealt = sb("w1_dealt", [P, PASSES * 2 * H], U8)
+        nc.vector.tensor_copy(
+            w1_dealt[:].bitcast(U16).rearrange("p (t g) -> p t g", t=PACK),
+            w1_raw[:].bitcast(U16).rearrange("p (g t) -> p t g", t=PACK),
+        )
 
         bgd = [sb(f"bgd{t}", [P, S], F32) for t in range(PACK)]
         total = sb("total", [P, PACK * GROUPS], F32)
@@ -119,33 +122,36 @@ def tile_picked_yfishm_log_p_kernel(
 
         for t in range(PACK):
             gather_bids(t, 0, False)
-            gather_bids(t, 1, t > 0)
+            gather_bids(t, 1, t % 2 == 1)
             add_pairs(t)
             if t > 0:
                 add_totals(t - 1)
         add_totals(PACK - 1)
 
+        unit_sb = sb("unit_sb", [P, PACK], F32, tag="bid0")
+        nc.sync.dma_start(unit_sb[:], unit.rearrange("(p t) o -> p (t o)", t=PACK))
+        w2_sb = sb("w2_sb", [P, 2 * N], U8, tag="bid1")
+        nc.sync.dma_start(w2_sb[:].bitcast(I32), w2_words[0].bitcast(I32))
+        w2s = sb("w2s", [P, N], U8, tag="bid2")
+        nc.vector.memset(w2s[:].bitcast(I32), 0)
+        for q in range(QUADS):
+            nc.sync.dma_start(w2s[32 * q : 32 * q + 4, :].bitcast(I32), w2_scales[0, 4 * q : 4 * q + 4, :].bitcast(I32))
+
         log_price = sb("log_price", [P, PACK * GROUPS], F32)
         last = (PACK - 1) * GROUPS
         nc.scalar.activation(log_price[:, :last], total[:, :last], ACT.Ln, bias=0.2)
         nc.scalar.activation(log_price[:, last:], total[:, last:], ACT.Ln, bias=0.2)
-        inv_price = sb("inv_price", [P, PACK * GROUPS], F32)
-        weight = sb("weight", [P, PACK * GROUPS], F32)
+        wide = {t: sb(f"wide{t}", [P, 2 * S], F32) for t in range(1, PACK)}
+        squashed0, val0, inv_price = (wide[t][:, S:] for t in range(1, PACK))
 
-        def half_groups(tile, h):
-            return tile[:].rearrange("p (t h v) -> p t h v", t=PACK, h=2)[:, :, h, :]
+        def half_groups(row, h):
+            return row.rearrange("p (t h v) -> p t h v", t=PACK, h=2)[:, :, h, :]
 
         for h in range(2):
-            nc.scalar.activation(half_groups(inv_price, h), half_groups(log_price, h), ACT.Exp, scale=-1.0)
-
-        w1_dealt = sb("w1_dealt", [P, PASSES * 2 * H], U8)
-        nc.vector.tensor_copy(
-            w1_dealt[:].bitcast(U16).rearrange("p (t g) -> p t g", t=PACK),
-            w1_raw[:].bitcast(U16).rearrange("p (g t) -> p t g", t=PACK),
-        )
+            nc.scalar.activation(half_groups(inv_price, h), half_groups(log_price[:], h), ACT.Exp, scale=-1.0)
 
         x_picked = [[sb(f"x_picked{o}_{h}", [P, HALF], U32) for h in range(2)] for o in range(PASSES)]
-        y = [[psum.tile([P, HALF], F32, name=f"y{t}_{h}", tag=f"bank{t}_{h}") for h in range(2)] for t in range(PACK)]
+        y = {}
 
         def gather_words(o, h):
             nc.vector.tensor_copy(
@@ -154,10 +160,13 @@ def tile_picked_yfishm_log_p_kernel(
 
         def first_product(o, t, h):
             blk = t * PASSES + o
+            if o == 0:
+                bank = (t - 2, 0) if (t >= 2 and h == 1) else (t, h)
+                y[t, h] = psum.tile([P, HALF], F32, name=f"y{t}_{h}", tag=f"bank{bank[0]}_{bank[1]}")
             nc.tensor.matmul_mx(
-                y[t][h][:],
+                y[t, h][:],
                 lhsT=w1_dealt[:, blk * 2 * P : (blk + 1) * 2 * P].bitcast(FP4X4),
-                lhsT_scale=w1s_planes[:, o * H + t * P : o * H + (t + 1) * P],
+                lhsT_scale=w1s_dealt[:, blk * P : (blk + 1) * P],
                 rhs=x_picked[o][h][:].bitcast(FP8X4),
                 rhs_scale=xs_planes[:, o * S + h * HALF : o * S + (h + 1) * HALF],
                 start=(o == 0),
@@ -166,21 +175,18 @@ def tile_picked_yfishm_log_p_kernel(
 
         for h in range(2):
             gather_words(0, h)
-            for t in range(PACK):
+            for t in range(PACK if h == 0 else 2):
                 first_product(0, t, h)
 
         for h in range(2):
-            nc.vector.tensor_tensor(half_groups(weight, h), half_groups(log_price, h), half_groups(inv_price, h), ALU.mult)
-
-        for h in range(2):
             gather_words(1, h)
-        for tp in range(2):
-            for h in range(2):
-                for t in (2 * tp, 2 * tp + 1):
-                    first_product(1, t, h)
+        for t, h in ((0, 0), (1, 0), (0, 1), (1, 1), (2, 0), (3, 0)):
+            first_product(1, t, h)
 
+        weight = sb("weight", [P, PACK * GROUPS], F32, tag="xs_table")
         factor = [sb(f"factor{h}", [P, PACK, HALF], F32) for h in range(2)]
         for h in range(2):
+            nc.vector.tensor_tensor(half_groups(weight[:], h), half_groups(log_price[:], h), half_groups(inv_price, h), ALU.mult)
             for t in range(PACK):
                 lo = t * GROUPS + h * (GROUPS // 2)
                 nc.vector.scalar_tensor_tensor(
@@ -192,40 +198,28 @@ def tile_picked_yfishm_log_p_kernel(
                     ALU.mult,
                 )
 
-        wide = [sb(f"wide{u}", [P, 2 * S], F32) for u in range(2)]
-        val = [sb(f"val{u}", [P, S], F32) for u in range(2)]
         vg = [sb(f"vg{h}", [P, PACK, HALF], F32) for h in range(2)]
 
         def squash(t, h):
-            lo = (S if t < 2 else 0) + h * HALF
-            nc.scalar.activation(wide[t % 2][:, lo : lo + HALF], y[t][h][:], ACT.Tanh)
-
-        def plain_exp(t):
-            nc.scalar.activation(val[t][:], wide[t][:, S:], ACT.Exp, scale=0.9)
-
-        def gather_val(t, h):
-            nc.vector.tensor_copy(vg[h][:, t, :], val[t][:].indirect(entries(good_sb, h * HALF, (h + 1) * HALF)))
-
-        def gather_exp(t, h):
-            nc.scalar.activation(
-                vg[h][:, t, :], wide[t % 2][:].indirect(entries(good_sb, h * HALF, (h + 1) * HALF)), ACT.Exp, scale=0.9
-            )
+            row = squashed0 if t == 0 else wide[t][:, :S]
+            nc.scalar.activation(row[:, h * HALF : (h + 1) * HALF], y[t, h][:], ACT.Tanh)
 
         squash(0, 0)
         squash(1, 0)
+        for t in range(2, PACK):
+            for o in range(PASSES):
+                first_product(o, t, 1)
         squash(0, 1)
-        plain_exp(0)
+        nc.scalar.activation(val0, squashed0, ACT.Exp, scale=0.9)
         squash(1, 1)
-        plain_exp(1)
-        for t in (2, 3):
+        for t in range(2, PACK):
             squash(t, 0)
             squash(t, 1)
-            gather_exp(t, 0)
-        for t in (2, 3):
-            gather_exp(t, 1)
-        for t in (0, 1):
-            for h in range(2):
-                gather_val(t, h)
+        for h in range(2):
+            half_list = entries(good_sb, h * HALF, (h + 1) * HALF)
+            nc.vector.tensor_copy(vg[h][:, 0, :], val0.indirect(half_list))
+            for t in range(1, PACK):
+                nc.scalar.activation(vg[h][:, t, :], wide[t][:].indirect(half_list), ACT.Exp, scale=0.9)
 
         pieces = [(0, 256), (256, 256), (512, 256), (768, 128), (896, 128)]
         for n, (lo, width) in enumerate(pieces):
@@ -240,7 +234,7 @@ def tile_picked_yfishm_log_p_kernel(
             codes = sb(f"codes{n}", [P, width], U32)
             scales = sb(f"scales{n}", [P, width], U8)
             nc.vector.quantize_mx(codes[:].bitcast(FP8X4), scales[:], hid[:])
-            acc = psum.tile([P, width], F32, name=f"acc{n}", tag=f"bank{n % PACK}_{n // PACK}")
+            acc = psum.tile([P, width], F32, name=f"acc{n}", tag=f"acc{n % 2}")
             nc.tensor.matmul_mx(
                 acc[:],
                 lhsT=w2_sb[:].bitcast(FP4X4),

@@ -51,6 +51,10 @@ def tile_picked_yfishm_log_p_kernel(
         nc.vector.memset(xs_table[0:TOP, :].bitcast(I32), 0)
         nc.vector.memset(xs_planes[:].bitcast(I32), 0)
 
+        warm = sb("warm", [P, 2], F32)
+        nc.gpsimd.memset(warm[:, 0:1], 1.0)
+        nc.scalar.activation(warm[:, 1:2], warm[:, 0:1], ACT.Ln)
+
         nc.sync.dma_start(offs_sb[:], offs)
         nc.sync.dma_start(xs_table[TOP:P, :].bitcast(I32), x_scales.bitcast(I32).rearrange("o s c -> s o c"))
         nc.sync.dma_start(good_sb[:], good)

@@ -20,10 +20,19 @@ P = 128
 PACK = 4
 PASSES = K // (P * PACK)
 HALF = S // 2
+QUARTER = S // 4
 GROUPS = S // D
-QUADS = 4
-LIST_COLS = S // 16
-TOP = 96
+QUADS, QUAD, SCALE_ROWS = 4, 32, 4
+LANES = 16
+LAST_QUAD = P - QUAD
+PRICE_FLOOR, TANH_GAIN = 0.2, 0.9
+
+BID_HALVES_ON_VECTOR = (1, 3)
+PLAIN = (0, 3)
+FUSED = (1, 2)
+PIECES = ((0, 256), (256, 256), (512, 256), (768, 128), (896, 128))
+ACC_BANKS = 2
+RUN = 2
 
 
 def tile_picked_yfishm_log_p_kernel(
@@ -38,37 +47,40 @@ def tile_picked_yfishm_log_p_kernel(
         def sb(name, shape, dtype, tag=None):
             return keep.tile(shape, dtype, name=name, tag=tag or name, align_bytes=64)
 
-        good_sb = lists.tile([P, LIST_COLS], U16, name="good_sb")
-        offs_sb = lists.tile([P, LIST_COLS], U16, name="offs_sb")
+        good_sb = lists.tile([P, S // LANES], U16, name="good_sb")
+        offs_sb = lists.tile([P, S // LANES], U16, name="offs_sb")
 
-        def entries(list_sb, lo, hi):
-            return list_sb[:, lo // 16 : hi // 16]
+        def entries(list_sb, first, count):
+            return list_sb[:, first // LANES : (first + count) // LANES]
+
+        def scale_rows(tile, q):
+            return tile[QUAD * q : QUAD * q + SCALE_ROWS, :].bitcast(I32)
 
         xs_table = sb("xs_table", [P, T], U8)
         w1s_raw = sb("w1s_raw", [P, PASSES * H], U8)
-        xs_planes = sb("xs_planes", [P, PASSES * S], U8)
+        xs_placed = sb("xs_placed", [P, PASSES * S], U8)
         nc.gpsimd.memset(w1s_raw[:].bitcast(I32), 0)
-        nc.vector.memset(xs_table[0:TOP, :].bitcast(I32), 0)
-        nc.vector.memset(xs_planes[:].bitcast(I32), 0)
+        nc.vector.memset(xs_table[0:LAST_QUAD, :].bitcast(I32), 0)
+        nc.vector.memset(xs_placed[:].bitcast(I32), 0)
 
         warm = sb("warm", [P, 2], F32)
         nc.gpsimd.memset(warm[:, 0:1], 1.0)
         nc.scalar.activation(warm[:, 1:2], warm[:, 0:1], ACT.Ln)
 
         nc.sync.dma_start(offs_sb[:], offs)
-        nc.sync.dma_start(xs_table[TOP:P, :].bitcast(I32), x_scales.bitcast(I32).rearrange("o s c -> s o c"))
+        nc.sync.dma_start(xs_table[LAST_QUAD:P, :].bitcast(I32), x_scales.bitcast(I32).rearrange("o s c -> s o c"))
         nc.sync.dma_start(good_sb[:], good)
-        bid_rows = bid.rearrange("(p t) j -> p t j", t=PACK)
+        bid_planes = bid.rearrange("(p t) j -> p t j", t=PACK)
         bid_sb = [sb(f"bid{t}", [P, S], F32) for t in range(PACK)]
-        for t in range(2):
-            nc.sync.dma_start(bid_sb[t][:], bid_rows[:, t, :])
+        for t in range(PACK // 2):
+            nc.sync.dma_start(bid_sb[t][:], bid_planes[:, t, :])
         for q in range(QUADS):
             nc.sync.dma_start(
-                w1s_raw[32 * q : 32 * q + 4, :].bitcast(I32).rearrange("r (o c) -> r o c", o=PASSES),
-                w1_scales[:, 4 * q : 4 * q + 4, :].bitcast(I32).rearrange("o r c -> r o c"),
+                scale_rows(w1s_raw, q).rearrange("r (o c) -> r o c", o=PASSES),
+                w1_scales[:, SCALE_ROWS * q : SCALE_ROWS * (q + 1), :].bitcast(I32).rearrange("o r c -> r o c"),
             )
-        for t in range(2, PACK):
-            nc.sync.dma_start(bid_sb[t][:], bid_rows[:, t, :])
+        for t in range(PACK // 2, PACK):
+            nc.sync.dma_start(bid_sb[t][:], bid_planes[:, t, :])
         w1_raw = sb("w1_raw", [P, PASSES * 2 * H], U8)
         nc.sync.dma_start(
             w1_raw[:].bitcast(I32).rearrange("p (o c) -> p o c", o=PASSES),
@@ -84,10 +96,11 @@ def tile_picked_yfishm_log_p_kernel(
 
         xs_picked = sb("xs_picked", [P, S], U8)
         nc.vector.tensor_copy(xs_picked[:], xs_table[:].indirect(offs_sb[:]))
+        moved_rows = SCALE_ROWS * PASSES
         for q in range(QUADS):
             nc.sync.dma_start(
-                xs_planes[32 * q : 32 * q + 4, :].bitcast(I32).rearrange("r (o c) -> r o c", o=PASSES),
-                xs_picked[TOP + 8 * q : TOP + 8 * q + 8, :].bitcast(I32),
+                scale_rows(xs_placed, q).rearrange("r (o c) -> r o c", o=PASSES),
+                xs_picked[LAST_QUAD + moved_rows * q : LAST_QUAD + moved_rows * (q + 1), :].bitcast(I32),
             )
         load_words(1, "xs_table")
 
@@ -96,20 +109,15 @@ def tile_picked_yfishm_log_p_kernel(
             w1s_dealt[:].rearrange("p (t g) -> p t g", t=PACK),
             w1s_raw[:].rearrange("p (g t) -> p t g", t=PACK),
         )
-        w1_dealt = sb("w1_dealt", [P, PASSES * 2 * H], U8)
-        nc.vector.tensor_copy(
-            w1_dealt[:].bitcast(U16).rearrange("p (t g) -> p t g", t=PACK),
-            w1_raw[:].bitcast(U16).rearrange("p (g t) -> p t g", t=PACK),
-        )
 
         bgd = [sb(f"bgd{t}", [P, S], F32) for t in range(PACK)]
         total = sb("total", [P, PACK * GROUPS], F32)
         pairs = [sb(f"pairs{t}", [P, 2 * GROUPS], F32) for t in range(PACK)]
 
-        def gather_bids(t, h, on_vector):
-            window = bid_sb[t][:].indirect(entries(good_sb, h * HALF, (h + 1) * HALF))
+        def gather_bids(t, h):
+            window = bid_sb[t][:].indirect(entries(good_sb, h * HALF, HALF))
             dst = bgd[t][:, h * HALF : (h + 1) * HALF]
-            if on_vector:
+            if h == 1 and t in BID_HALVES_ON_VECTOR:
                 nc.vector.tensor_copy(dst, window)
             else:
                 nc.scalar.activation(dst, window, ACT.Copy)
@@ -125,12 +133,18 @@ def tile_picked_yfishm_log_p_kernel(
             nc.vector.tensor_tensor(total[:, t * GROUPS : (t + 1) * GROUPS], two[:, :, 0], two[:, :, 1], ALU.add)
 
         for t in range(PACK):
-            gather_bids(t, 0, False)
-            gather_bids(t, 1, t % 2 == 1)
+            gather_bids(t, 0)
+            gather_bids(t, 1)
             add_pairs(t)
             if t > 0:
                 add_totals(t - 1)
         add_totals(PACK - 1)
+
+        w1_dealt = sb("w1_dealt", [P, PASSES * 2 * H], U8, tag=f"pairs{PACK - 1}")
+        nc.vector.tensor_copy(
+            w1_dealt[:].bitcast(U16).rearrange("p (t g) -> p t g", t=PACK),
+            w1_raw[:].bitcast(U16).rearrange("p (g t) -> p t g", t=PACK),
+        )
 
         unit_sb = sb("unit_sb", [P, PACK], F32, tag="bid0")
         nc.sync.dma_start(unit_sb[:], unit.rearrange("(p t) o -> p (t o)", t=PACK))
@@ -139,106 +153,123 @@ def tile_picked_yfishm_log_p_kernel(
         w2s = sb("w2s", [P, N], U8, tag="bid2")
         nc.vector.memset(w2s[:].bitcast(I32), 0)
         for q in range(QUADS):
-            nc.sync.dma_start(w2s[32 * q : 32 * q + 4, :].bitcast(I32), w2_scales[0, 4 * q : 4 * q + 4, :].bitcast(I32))
+            nc.sync.dma_start(scale_rows(w2s, q), w2_scales[0, SCALE_ROWS * q : SCALE_ROWS * (q + 1), :].bitcast(I32))
 
         log_price = sb("log_price", [P, PACK * GROUPS], F32)
-        last = (PACK - 1) * GROUPS
-        nc.scalar.activation(log_price[:, :last], total[:, :last], ACT.Ln, bias=0.2)
-        nc.scalar.activation(log_price[:, last:], total[:, last:], ACT.Ln, bias=0.2)
-        wide = {t: sb(f"wide{t}", [P, 2 * S], F32) for t in range(1, PACK)}
-        squashed0, val0, inv_price = (wide[t][:, S:] for t in range(1, PACK))
+        last_plane = (PACK - 1) * GROUPS
+        nc.scalar.activation(log_price[:, :last_plane], total[:, :last_plane], ACT.Ln, bias=PRICE_FLOOR)
+        nc.scalar.activation(log_price[:, last_plane:], total[:, last_plane:], ACT.Ln, bias=PRICE_FLOOR)
+        inv_price = sb("inv_price", [P, PACK * GROUPS], F32)
 
-        def half_groups(row, h):
-            return row.rearrange("p (t h v) -> p t h v", t=PACK, h=2)[:, :, h, :]
+        def half_groups(tile, h):
+            return tile[:].rearrange("p (t h v) -> p t h v", t=PACK, h=2)[:, :, h, :]
 
         for h in range(2):
-            nc.scalar.activation(half_groups(inv_price, h), half_groups(log_price[:], h), ACT.Exp, scale=-1.0)
+            nc.scalar.activation(half_groups(inv_price, h), half_groups(log_price, h), ACT.Exp, scale=-1.0)
 
         x_picked = [[sb(f"x_picked{o}_{h}", [P, HALF], U32) for h in range(2)] for o in range(PASSES)]
         y = {}
 
         def gather_words(o, h):
             nc.vector.tensor_copy(
-                x_picked[o][h][:], x_table[o][:].bitcast(U32).indirect(entries(offs_sb, h * HALF, (h + 1) * HALF))
+                x_picked[o][h][:], x_table[o][:].bitcast(U32).indirect(entries(offs_sb, h * HALF, HALF))
             )
 
         def first_product(o, t, h):
-            blk = t * PASSES + o
+            block = t * PASSES + o
             if o == 0:
-                bank = (t - 2, 0) if (t >= 2 and h == 1) else (t, h)
+                bank = (PLAIN[FUSED.index(t)], 0) if (t in FUSED and h == 1) else (t, h)
                 y[t, h] = psum.tile([P, HALF], F32, name=f"y{t}_{h}", tag=f"bank{bank[0]}_{bank[1]}")
             nc.tensor.matmul_mx(
                 y[t, h][:],
-                lhsT=w1_dealt[:, blk * 2 * P : (blk + 1) * 2 * P].bitcast(FP4X4),
-                lhsT_scale=w1s_dealt[:, blk * P : (blk + 1) * P],
+                lhsT=w1_dealt[:, block * 2 * P : (block + 1) * 2 * P].bitcast(FP4X4),
+                lhsT_scale=w1s_dealt[:, block * P : (block + 1) * P],
                 rhs=x_picked[o][h][:].bitcast(FP8X4),
-                rhs_scale=xs_planes[:, o * S + h * HALF : o * S + (h + 1) * HALF],
+                rhs_scale=xs_placed[:, o * S + h * HALF : o * S + (h + 1) * HALF],
                 start=(o == 0),
                 stop=(o == PASSES - 1),
             )
 
         for h in range(2):
             gather_words(0, h)
-            for t in range(PACK if h == 0 else 2):
+            for t in PLAIN + FUSED if h == 0 else PLAIN:
                 first_product(0, t, h)
 
+        weight = [None, None]
+
+        def make_weight(h, tag):
+            weight[h] = sb(f"weight{h}", [P, PACK, GROUPS // 2], F32, tag=tag)
+            nc.vector.tensor_tensor(weight[h][:], half_groups(log_price, h), half_groups(inv_price, h), ALU.mult)
+
+        make_weight(0, "x_table0")
         for h in range(2):
             gather_words(1, h)
-        for t, h in ((0, 0), (1, 0), (0, 1), (1, 1), (2, 0), (3, 0)):
-            first_product(1, t, h)
+        for h in range(2):
+            for t in PLAIN:
+                first_product(1, t, h)
+        for t in FUSED:
+            first_product(1, t, 0)
 
-        weight = sb("weight", [P, PACK * GROUPS], F32, tag="xs_table")
         factor = [sb(f"factor{h}", [P, PACK, HALF], F32) for h in range(2)]
         for h in range(2):
-            nc.vector.tensor_tensor(half_groups(weight[:], h), half_groups(log_price[:], h), half_groups(inv_price, h), ALU.mult)
+            if h == 1:
+                make_weight(1, "xs_table")
             for t in range(PACK):
-                lo = t * GROUPS + h * (GROUPS // 2)
                 nc.vector.scalar_tensor_tensor(
                     factor[h][:, t, :].rearrange("p (v d) -> p v d", d=D),
                     bgd[t][:, h * HALF : (h + 1) * HALF].rearrange("p (v d) -> p v d", d=D),
                     unit_sb[:, t : t + 1],
-                    weight[:, lo : lo + GROUPS // 2].unsqueeze(2).to_broadcast([P, GROUPS // 2, D]),
+                    weight[h][:, t, :].unsqueeze(2).to_broadcast([P, GROUPS // 2, D]),
                     ALU.mult,
                     ALU.mult,
                 )
 
+        wide = [sb(f"wide{u}", [P, 2 * S], F32) for u in range(2)]
+        squashed = {}
+        for u in range(2):
+            squashed[FUSED[u]] = wide[u][:, :S]
+            squashed[PLAIN[u]] = wide[u][:, S:]
+        val = {t: sb(f"val{t}", [P, S], F32) for t in PLAIN}
         vg = [sb(f"vg{h}", [P, PACK, HALF], F32) for h in range(2)]
 
         def squash(t, h):
-            row = squashed0 if t == 0 else wide[t][:, :S]
-            nc.scalar.activation(row[:, h * HALF : (h + 1) * HALF], y[t, h][:], ACT.Tanh)
+            nc.scalar.activation(squashed[t][:, h * HALF : (h + 1) * HALF], y[t, h][:], ACT.Tanh)
 
-        squash(0, 0)
-        squash(1, 0)
-        for t in range(2, PACK):
+        for t in PLAIN:
+            squash(t, 0)
+        for t in FUSED:
             for o in range(PASSES):
                 first_product(o, t, 1)
-        squash(0, 1)
-        nc.scalar.activation(val0, squashed0, ACT.Exp, scale=0.9)
-        squash(1, 1)
-        for t in range(2, PACK):
+        for t in PLAIN:
+            squash(t, 1)
+            nc.scalar.activation(val[t][:], squashed[t], ACT.Exp, scale=TANH_GAIN)
+        for t in FUSED:
             squash(t, 0)
             squash(t, 1)
         for h in range(2):
-            half_list = entries(good_sb, h * HALF, (h + 1) * HALF)
-            nc.vector.tensor_copy(vg[h][:, 0, :], val0.indirect(half_list))
-            for t in range(1, PACK):
-                nc.scalar.activation(vg[h][:, t, :], wide[t][:].indirect(half_list), ACT.Exp, scale=0.9)
+            half_list = entries(good_sb, h * HALF, HALF)
+            for t in PLAIN if h == 0 else PLAIN[:-1]:
+                nc.vector.tensor_copy(vg[h][:, t, :], val[t][:].indirect(half_list))
+            for u, t in enumerate(FUSED):
+                nc.scalar.activation(vg[h][:, t, :], wide[u][:].indirect(half_list), ACT.Exp, scale=TANH_GAIN)
+        t = PLAIN[-1]
+        for c0 in (0, QUARTER):
+            quarter_list = entries(good_sb, HALF + c0, QUARTER)
+            nc.scalar.activation(vg[1][:, t, c0 : c0 + QUARTER], val[t][:].indirect(quarter_list), ACT.Copy)
 
-        pieces = [(0, 256), (256, 256), (512, 256), (768, 128), (896, 128)]
-        for n, (lo, width) in enumerate(pieces):
-            h, c0 = divmod(lo, HALF)
+        for n, (first, width) in enumerate(PIECES):
+            h, c0 = divmod(first, HALF)
             hid = sb(f"hid{n}", [P, PACK * width], BF16)
             nc.vector.tensor_tensor(
-                hid[:].rearrange("p (c i t) -> p c t i", i=2, t=PACK),
-                vg[h][:, :, c0 : c0 + width].rearrange("p t (c i) -> p c t i", i=2),
-                factor[h][:, :, c0 : c0 + width].rearrange("p t (c i) -> p c t i", i=2),
+                hid[:].rearrange("p (c e t) -> p c t e", e=RUN, t=PACK),
+                vg[h][:, :, c0 : c0 + width].rearrange("p t (c e) -> p c t e", e=RUN),
+                factor[h][:, :, c0 : c0 + width].rearrange("p t (c e) -> p c t e", e=RUN),
                 ALU.mult,
             )
             codes = sb(f"codes{n}", [P, width], U32)
             scales = sb(f"scales{n}", [P, width], U8)
             nc.vector.quantize_mx(codes[:].bitcast(FP8X4), scales[:], hid[:])
-            acc = psum.tile([P, width], F32, name=f"acc{n}", tag=f"acc{n % 2}")
+            acc = psum.tile([P, width], F32, name=f"acc{n}", tag=f"acc{n % ACC_BANKS}")
             nc.tensor.matmul_mx(
                 acc[:],
                 lhsT=w2_sb[:].bitcast(FP4X4),
@@ -250,4 +281,4 @@ def tile_picked_yfishm_log_p_kernel(
             )
             res = sb(f"res{n}", [P, width], F32)
             nc.scalar.copy(res[:], acc[:])
-            nc.sync.dma_start(out[:, lo : lo + width], res[:])
+            nc.sync.dma_start(out[:, first : first + width], res[:])

from contextlib import ExitStack

import concourse.mybir as mybir

K, T, S, D, N, H = 1024, 4096, 1024, 4, 128, 512
FLOPS = 2 * K * H * S + 2 * H * N * S

F32 = mybir.dt.float32
BF16 = mybir.dt.bfloat16
I32 = mybir.dt.int32
U32 = mybir.dt.uint32
U16 = mybir.dt.uint16
U8 = mybir.dt.uint8
FP8X4 = mybir.dt.float8_e4m3fn_x4
FP4X4 = mybir.dt.float4_e2m1fn_x4
ACT = mybir.ActivationFunctionType
ALU = mybir.AluOpType

P = 128
PACK = 4
PASSES = K // (P * PACK)
HALF = S // 2
QUARTER = S // 4
GROUPS = S // D
QUADS, QUAD, SCALE_ROWS = 4, 32, 4
LANES = 16
LAST_QUAD = P - QUAD
PRICE_FLOOR, TANH_GAIN = 0.2, 0.9

BID_HALVES_ON_VECTOR = (1, 3)
PLAIN = (0, 3)
FUSED = (1, 2)
PIECES = ((0, 256), (256, 256), (512, 256), (768, 128), (896, 128))
ACC_BANKS = 2
RUN = 2


def tile_picked_yfishm_log_p_kernel(
    tc, x_words, x_scales, w1_words, w1_scales, bid, unit, w2_words, w2_scales, offs, good, out
):
    nc = tc.nc
    with ExitStack() as ctx:
        lists = ctx.enter_context(tc.tile_pool(name="lists", bufs=1))
        keep = ctx.enter_context(tc.tile_pool(name="keep", bufs=1))
        psum = ctx.enter_context(tc.psum_pool(name="psum", bufs=1))

        def sb(name, shape, dtype, tag=None):
            return keep.tile(shape, dtype, name=name, tag=tag or name, align_bytes=64)

        good_sb = lists.tile([P, S // LANES], U16, name="good_sb")
        offs_sb = lists.tile([P, S // LANES], U16, name="offs_sb")

        def entries(list_sb, first, count):
            return list_sb[:, first // LANES : (first + count) // LANES]

        def scale_rows(tile, q):
            return tile[QUAD * q : QUAD * q + SCALE_ROWS, :].bitcast(I32)

        xs_table = sb("xs_table", [P, T], U8)
        w1s_raw = sb("w1s_raw", [P, PASSES * H], U8)
        xs_placed = sb("xs_placed", [P, PASSES * S], U8)
        nc.gpsimd.memset(w1s_raw[:].bitcast(I32), 0)
        nc.vector.memset(xs_table[0:LAST_QUAD, :].bitcast(I32), 0)
        nc.vector.memset(xs_placed[:].bitcast(I32), 0)

        warm = sb("warm", [P, 2], F32)
        nc.gpsimd.memset(warm[:, 0:1], 1.0)
        nc.scalar.activation(warm[:, 1:2], warm[:, 0:1], ACT.Ln)

        nc.sync.dma_start(offs_sb[:], offs)
        nc.sync.dma_start(xs_table[LAST_QUAD:P, :].bitcast(I32), x_scales.bitcast(I32).rearrange("o s c -> s o c"))
        nc.sync.dma_start(good_sb[:], good)
        bid_planes = bid.rearrange("(p t) j -> p t j", t=PACK)
        bid_sb = [sb(f"bid{t}", [P, S], F32) for t in range(PACK)]
        for t in range(PACK // 2):
            nc.sync.dma_start(bid_sb[t][:], bid_planes[:, t, :])
        for q in range(QUADS):
            nc.sync.dma_start(
                scale_rows(w1s_raw, q).rearrange("r (o c) -> r o c", o=PASSES),
                w1_scales[:, SCALE_ROWS * q : SCALE_ROWS * (q + 1), :].bitcast(I32).rearrange("o r c -> r o c"),
            )
        for t in range(PACK // 2, PACK):
            nc.sync.dma_start(bid_sb[t][:], bid_planes[:, t, :])
        w1_raw = sb("w1_raw", [P, PASSES * 2 * H], U8)
        nc.sync.dma_start(
            w1_raw[:].bitcast(I32).rearrange("p (o c) -> p o c", o=PASSES),
            w1_words.bitcast(I32).rearrange("o p c -> p o c"),
        )
        x_table = [None] * PASSES

        def load_words(o, tag):
            x_table[o] = sb(f"x_table{o}", [P, T], I32, tag=tag)
            nc.sync.dma_start(x_table[o][:], x_words[o].rearrange("p c r -> p (c r)").bitcast(I32))

        load_words(0, "x_table0")

        xs_picked = sb("xs_picked", [P, S], U8)
        nc.vector.tensor_copy(xs_picked[:], xs_table[:].indirect(offs_sb[:]))
        moved_rows = SCALE_ROWS * PASSES
        for q in range(QUADS):
            nc.sync.dma_start(
                scale_rows(xs_placed, q).rearrange("r (o c) -> r o c", o=PASSES),
                xs_picked[LAST_QUAD + moved_rows * q : LAST_QUAD + moved_rows * (q + 1), :].bitcast(I32),
            )
        load_words(1, "xs_table")

        w1s_dealt = sb("w1s_dealt", [P, PASSES * H], U8)
        nc.vector.tensor_copy(
            w1s_dealt[:].rearrange("p (t g) -> p t g", t=PACK),
            w1s_raw[:].rearrange("p (g t) -> p t g", t=PACK),
        )

        bgd = [sb(f"bgd{t}", [P, S], F32) for t in range(PACK)]
        total = sb("total", [P, PACK * GROUPS], F32)
        pairs = [sb(f"pairs{t}", [P, 2 * GROUPS], F32) for t in range(PACK)]

        def gather_bids(t, h):
            window = bid_sb[t][:].indirect(entries(good_sb, h * HALF, HALF))
            dst = bgd[t][:, h * HALF : (h + 1) * HALF]
            if h == 1 and t in BID_HALVES_ON_VECTOR:
                nc.vector.tensor_copy(dst, window)
            else:
                nc.scalar.activation(dst, window, ACT.Copy)

        def add_pairs(t):
            four = bgd[t][:].rearrange("p (v d) -> p v d", d=D)
            nc.vector.tensor_tensor(
                pairs[t][:].rearrange("p (v e) -> p v e", e=2), four[:, :, 0:2], four[:, :, 2:4], ALU.add
            )

        def add_totals(t):
            two = pairs[t][:].rearrange("p (v e) -> p v e", e=2)
            nc.vector.tensor_tensor(total[:, t * GROUPS : (t + 1) * GROUPS], two[:, :, 0], two[:, :, 1], ALU.add)

        for t in range(PACK):
            gather_bids(t, 0)
            gather_bids(t, 1)
            add_pairs(t)
            if t > 0:
                add_totals(t - 1)
        add_totals(PACK - 1)

        w1_dealt = sb("w1_dealt", [P, PASSES * 2 * H], U8, tag=f"pairs{PACK - 1}")
        nc.vector.tensor_copy(
            w1_dealt[:].bitcast(U16).rearrange("p (t g) -> p t g", t=PACK),
            w1_raw[:].bitcast(U16).rearrange("p (g t) -> p t g", t=PACK),
        )

        unit_sb = sb("unit_sb", [P, PACK], F32, tag="bid0")
        nc.sync.dma_start(unit_sb[:], unit.rearrange("(p t) o -> p (t o)", t=PACK))
        w2_sb = sb("w2_sb", [P, 2 * N], U8, tag="bid1")
        nc.sync.dma_start(w2_sb[:].bitcast(I32), w2_words[0].bitcast(I32))
        w2s = sb("w2s", [P, N], U8, tag="bid2")
        nc.vector.memset(w2s[:].bitcast(I32), 0)
        for q in range(QUADS):
            nc.sync.dma_start(scale_rows(w2s, q), w2_scales[0, SCALE_ROWS * q : SCALE_ROWS * (q + 1), :].bitcast(I32))

        log_price = sb("log_price", [P, PACK * GROUPS], F32)
        last_plane = (PACK - 1) * GROUPS
        nc.scalar.activation(log_price[:, :last_plane], total[:, :last_plane], ACT.Ln, bias=PRICE_FLOOR)
        nc.scalar.activation(log_price[:, last_plane:], total[:, last_plane:], ACT.Ln, bias=PRICE_FLOOR)
        inv_price = sb("inv_price", [P, PACK * GROUPS], F32)

        def half_groups(tile, h):
            return tile[:].rearrange("p (t h v) -> p t h v", t=PACK, h=2)[:, :, h, :]

        for h in range(2):
            nc.scalar.activation(half_groups(inv_price, h), half_groups(log_price, h), ACT.Exp, scale=-1.0)

        x_picked = [[sb(f"x_picked{o}_{h}", [P, HALF], U32) for h in range(2)] for o in range(PASSES)]
        y = {}

        def gather_words(o, h):
            nc.vector.tensor_copy(
                x_picked[o][h][:], x_table[o][:].bitcast(U32).indirect(entries(offs_sb, h * HALF, HALF))
            )

        def first_product(o, t, h):
            block = t * PASSES + o
            if o == 0:
                bank = (PLAIN[FUSED.index(t)], 0) if (t in FUSED and h == 1) else (t, h)
                y[t, h] = psum.tile([P, HALF], F32, name=f"y{t}_{h}", tag=f"bank{bank[0]}_{bank[1]}")
            nc.tensor.matmul_mx(
                y[t, h][:],
                lhsT=w1_dealt[:, block * 2 * P : (block + 1) * 2 * P].bitcast(FP4X4),
                lhsT_scale=w1s_dealt[:, block * P : (block + 1) * P],
                rhs=x_picked[o][h][:].bitcast(FP8X4),
                rhs_scale=xs_placed[:, o * S + h * HALF : o * S + (h + 1) * HALF],
                start=(o == 0),
                stop=(o == PASSES - 1),
            )

        for h in range(2):
            gather_words(0, h)
            for t in PLAIN + FUSED if h == 0 else PLAIN:
                first_product(0, t, h)

        weight = [None, None]

        def make_weight(h, tag):
            weight[h] = sb(f"weight{h}", [P, PACK, GROUPS // 2], F32, tag=tag)
            nc.vector.tensor_tensor(weight[h][:], half_groups(log_price, h), half_groups(inv_price, h), ALU.mult)

        make_weight(0, "x_table0")
        for h in range(2):
            gather_words(1, h)
        for h in range(2):
            for t in PLAIN:
                first_product(1, t, h)
        for t in FUSED:
            first_product(1, t, 0)

        factor = [sb(f"factor{h}", [P, PACK, HALF], F32) for h in range(2)]
        for h in range(2):
            if h == 1:
                make_weight(1, "xs_table")
            for t in range(PACK):
                nc.vector.scalar_tensor_tensor(
                    factor[h][:, t, :].rearrange("p (v d) -> p v d", d=D),
                    bgd[t][:, h * HALF : (h + 1) * HALF].rearrange("p (v d) -> p v d", d=D),
                    unit_sb[:, t : t + 1],
                    weight[h][:, t, :].unsqueeze(2).to_broadcast([P, GROUPS // 2, D]),
                    ALU.mult,
                    ALU.mult,
                )

        wide = [sb(f"wide{u}", [P, 2 * S], F32) for u in range(2)]
        squashed = {}
        for u in range(2):
            squashed[FUSED[u]] = wide[u][:, :S]
            squashed[PLAIN[u]] = wide[u][:, S:]
        val = {t: sb(f"val{t}", [P, S], F32) for t in PLAIN}
        vg = [sb(f"vg{h}", [P, PACK, HALF], F32) for h in range(2)]

        def squash(t, h):
            nc.scalar.activation(squashed[t][:, h * HALF : (h + 1) * HALF], y[t, h][:], ACT.Tanh)

        for t in PLAIN:
            squash(t, 0)
        for t in FUSED:
            for o in range(PASSES):
                first_product(o, t, 1)
        for t in PLAIN:
            squash(t, 1)
            nc.scalar.activation(val[t][:], squashed[t], ACT.Exp, scale=TANH_GAIN)
        for t in FUSED:
            squash(t, 0)
            squash(t, 1)
        for h in range(2):
            half_list = entries(good_sb, h * HALF, HALF)
            for t in PLAIN if h == 0 else PLAIN[:-1]:
                nc.vector.tensor_copy(vg[h][:, t, :], val[t][:].indirect(half_list))
            for u, t in enumerate(FUSED):
                nc.scalar.activation(vg[h][:, t, :], wide[u][:].indirect(half_list), ACT.Exp, scale=TANH_GAIN)
        t = PLAIN[-1]
        for c0 in (0, QUARTER):
            quarter_list = entries(good_sb, HALF + c0, QUARTER)
            nc.scalar.activation(vg[1][:, t, c0 : c0 + QUARTER], val[t][:].indirect(quarter_list), ACT.Copy)

        for n, (first, width) in enumerate(PIECES):
            h, c0 = divmod(first, HALF)
            hid = sb(f"hid{n}", [P, PACK * width], BF16)
            nc.vector.tensor_tensor(
                hid[:].rearrange("p (c e t) -> p c t e", e=RUN, t=PACK),
                vg[h][:, :, c0 : c0 + width].rearrange("p t (c e) -> p c t e", e=RUN),
                factor[h][:, :, c0 : c0 + width].rearrange("p t (c e) -> p c t e", e=RUN),
                ALU.mult,
            )
            codes = sb(f"codes{n}", [P, width], U32)
            scales = sb(f"scales{n}", [P, width], U8)
            nc.vector.quantize_mx(codes[:].bitcast(FP8X4), scales[:], hid[:])
            acc = psum.tile([P, width], F32, name=f"acc{n}", tag=f"acc{n % ACC_BANKS}")
            nc.tensor.matmul_mx(
                acc[:],
                lhsT=w2_sb[:].bitcast(FP4X4),
                lhsT_scale=w2s[:],
                rhs=codes[:].bitcast(FP8X4),
                rhs_scale=scales[:],
                start=True,
                stop=True,
            )
            res = sb(f"res{n}", [P, width], F32)
            nc.scalar.copy(res[:], acc[:])
            nc.sync.dma_start(out[:, first : first + width], res[:])
